import numpy as np
import ml_dtypes


def mxq(x, axis, fmt="e4m3"):
    dtype, down = {"e4m3": (ml_dtypes.float8_e4m3fn, 7), "e5m2": (ml_dtypes.float8_e5m2, 14)}[fmt]
    v = np.moveaxis(np.asarray(x, np.float32).astype(ml_dtypes.bfloat16).astype(np.float64), axis, -1)
    blocks = v.reshape(v.shape[:-1] + (-1, 32))
    amax = np.abs(blocks).max(-1, keepdims=True)
    byte = np.maximum(np.where(amax > 0, np.frexp(amax)[1] - 1 + 127, 0) - down, 1)
    scale = np.exp2(byte - 127.0)
    codes = (blocks / scale).astype(np.float32).astype(dtype).astype(np.float64)
    return np.moveaxis((codes * scale).reshape(v.shape), -1, axis)


WIDE = False


def mx_kscale(k):
    if not WIDE:
        return np.ones(k)
    levels = np.array([10, -10, 5, -5, 0])
    if k % 512:
        return np.exp2(np.random.permutation(np.resize(levels, k // 32))).repeat(32)
    a = np.empty((k // 512, 16))
    for p in range(k // 512):
        a[p, :8] = np.random.permutation(np.resize(levels, 8))
        for g in range(8):
            far = levels[np.abs(levels - a[p, g]) >= 10]
            a[p, g + 8] = far[np.random.randint(len(far))]
    return np.exp2(a.ravel()).repeat(32)


def f64(x):
    return np.asarray(x).astype(np.float64)


def striped(idx):
    return np.tile(idx.reshape(-1, 16).T, (8, 1)).astype(np.uint16)


def unstriped(offs):
    return offs[:16].T.reshape(-1).astype(np.int64)


E2M1 = np.array([0.0, 0.5, 1.0, 1.5, 2.0, 3.0, 4.0, 6.0, -0.0, -0.5, -1.0, -1.5, -2.0, -3.0, -4.0, -6.0])


def pack_weight(w, fmt):
    k, n = w.shape
    w = f64(np.asarray(w, np.float32).astype(ml_dtypes.bfloat16)).reshape(k // 32, 32, n)
    amax = np.abs(w).max(1)
    if fmt == "e4m3":
        byte = np.frexp(amax)[1] - 1 + 127 - 7
    else:
        mant, ex = np.frexp(amax / 6.0)
        byte = np.where(mant > 0.5, ex, ex - 1) + 127
    byte = np.clip(np.where(amax > 0, byte, 1), 1, 254)
    scaled = (w * np.exp2(127.0 - byte)[:, None, :]).reshape(k, n).astype(np.float32)
    by_word = np.ascontiguousarray(scaled.reshape(k // 512, 128, 4, n).transpose(0, 1, 3, 2))
    if fmt == "e4m3":
        words = by_word.astype(ml_dtypes.float8_e4m3fn).view(np.uint8)
    else:
        c = by_word.astype(ml_dtypes.float4_e2m1fn).view(np.uint8) & 0xF
        words = (c[..., 0::2] | (c[..., 1::2] << 4)).reshape(k // 512, 128, 2 * n)
    return np.ascontiguousarray(words), np.ascontiguousarray(byte.astype(np.uint8).reshape(k // 512, 16, n))


def unpack_weight(words, scales, fmt):
    g, _, n = scales.shape
    words = np.ascontiguousarray(words).reshape(g, 128, n, -1)
    if fmt == "e4m3":
        vals = words.view(ml_dtypes.float8_e4m3fn).astype(np.float64)
    else:
        nib = np.empty((g, 128, n, 4), np.uint8)
        nib[..., 0::2] = words & 0xF
        nib[..., 1::2] = words >> 4
        vals = E2M1[nib]
    vals = vals * np.repeat(np.exp2(scales.astype(np.float64) - 127.0), 8, axis=1)[..., None]
    return vals.transpose(0, 1, 3, 2).reshape(g * 512, n)


def gelu(v):
    return 0.5 * v * (1.0 + np.tanh(np.sqrt(2.0 / np.pi) * (v + 0.044715 * v**3)))


def twice(P):
    return np.random.permutation(np.repeat(np.arange(P), 2))


K, T, S, P, H = 512, 4096, 1024, 512, 1024

def setup_inputs():
    n = np.random.standard_normal
    s = mx_kscale(K)[:, None]
    u = mx_kscale(H)[:, None]
    d = {}
    d["tab_words"], d["tab_scales"] = pack_weight(n((K, T)) * s, "e4m3")
    d["offs"] = striped(np.random.permutation(T)[:S])
    d["pos1"] = striped(np.random.permutation(S)[:P])
    d["pos2"] = striped(np.random.permutation(S)[:P])
    d["pos3"] = striped(twice(P))
    d["w1"] = (1.5 * n((K, H)) / K ** 0.5 / s * u.T).astype(np.float32)
    d["w2_words"], d["w2_scales"] = pack_weight(1.5 * n((K, H)) / K ** 0.5 / s * u.T, "e2m1")
    d["bias"] = ((0.8 * n(H) - 0.6) * u[:, 0]).astype(np.float32)
    d["unit"] = (np.exp(0.3 * n(H)) * u[:, 0] ** 2).astype(np.float32)
    d["w3"] = (n((H, H)) / H ** 0.5 / u).astype(np.float32)
    d["gain"] = (np.exp(0.3 * n(H)) / u[:, 0]).astype(np.float32)
    return d

def reference(tab_words, tab_scales, offs, pos1, pos2, pos3, w1, w2_words, w2_scales, bias, unit, w3, gain):
    v = unpack_weight(tab_words, tab_scales, "e4m3")[:, unstriped(offs)]
    w2 = unpack_weight(w2_words, w2_scales, "e2m1")
    a = np.abs(mxq(f64(w1), 0, "e4m3").T @ v)
    h = a + (w2.T @ v) + f64(bias)[:, None]
    diff = h[:, unstriped(pos1)] - h[:, unstriped(pos2)]
    z = np.sqrt(f64(unit)[:, None] + np.square(diff))
    y = mxq(f64(w3), 0, "e4m3").T @ mxq(z, 0, "e4m3")
    return np.minimum(y[:, unstriped(pos3)], f64(gain)[:, None] * h)

@@ -1,0 +1,259 @@
+from contextlib import ExitStack
+
+import concourse.mybir as mybir
+
+K, T, S, PAIRS, H = 512, 4096, 1024, 512, 1024
+FLOPS = 2 * (2 * K * H * S + H * H * PAIRS)
+
+F32 = mybir.dt.float32
+BF16 = mybir.dt.bfloat16
+I32 = mybir.dt.int32
+U32 = mybir.dt.uint32
+U16 = mybir.dt.uint16
+U8 = mybir.dt.uint8
+FP8X4 = mybir.dt.float8_e4m3fn_x4
+FP4X4 = mybir.dt.float4_e2m1fn_x4
+ALU = mybir.AluOpType
+ACT = mybir.ActivationFunctionType
+
+P = 128
+PACK = 4
+PASS = P * PACK
+BANK = 512
+GROUPS = H // PASS
+TILES = H // P
+LIST_ROWS = 16
+
+
+def load_scale_rows(queue, plane, scales):
+    for q in range(4):
+        queue.dma_start(
+            out=plane[32 * q : 32 * q + 4, :].bitcast(I32),
+            in_=scales[0, 4 * q : 4 * q + 4, :].bitcast(I32),
+        )
+
+
+def round_and_deal(nc, grouped, raw, pair):
+    nc.scalar.copy(
+        out=grouped.rearrange("p (t m j) -> p m j t", t=2, j=PACK),
+        in_=raw[:].rearrange("p j (m t) -> p m j t", t=PACK)[:, :, :, 2 * pair : 2 * pair + 2],
+    )
+
+
+def tile_list_raceway_noise_scores_kernel(
+    tc, tab_words, tab_scales, offs, pos1, pos2, pos3, w1, w2_words, w2_scales, bias, unit, w3, gain, out
+):
+    nc = tc.nc
+    with ExitStack() as ctx:
+        keep = ctx.enter_context(tc.tile_pool(name="keep", bufs=1))
+        ring = ctx.enter_context(tc.tile_pool(name="ring", bufs=2))
+        psum = ctx.enter_context(tc.psum_pool(name="psum", bufs=4))
+
+        idx = keep.tile([P, S // LIST_ROWS], U16, name="idx")
+        p1 = keep.tile([P, PAIRS // LIST_ROWS], U16, name="p1")
+        p2 = keep.tile([P, PAIRS // LIST_ROWS], U16, name="p2")
+        p3 = keep.tile([P, S // LIST_ROWS], U16, name="p3")
+        tab_w = keep.tile([P, T], U32, name="tab_w", align_bytes=64)
+        tab_s = keep.tile([P, T], U8, name="tab_s", align_bytes=64)
+        w2_w = keep.tile([P, 2 * H], U8, name="w2_w", align_bytes=64)
+        w2_s = keep.tile([P, H], U8, name="w2_s", align_bytes=64)
+        w1_raw = [keep.tile([P, PACK, PASS], F32, name="w1_raw%d" % b) for b in range(GROUPS)]
+        w3_raw = [
+            [keep.tile([P, PACK, PASS], F32, name="w3_raw%d%d" % (a, b)) for b in range(GROUPS)]
+            for a in range(GROUPS)
+        ]
+        bias_c = keep.tile([P, GROUPS, PACK], F32, name="bias_c")
+        unit_c = keep.tile([P, GROUPS, PACK], F32, name="unit_c")
+        gain_c = keep.tile([P, GROUPS, PACK], F32, name="gain_c")
+
+        tab_s_words = tab_s[:].bitcast(I32)
+        nc.vector.memset(tab_s_words[:, 0 : T // 8], 0)
+        nc.gpsimd.memset(tab_s_words[:, T // 8 : T // 4], 0)
+        nc.vector.memset(w2_s[:].bitcast(I32), 0)
+
+        w1_rows = w1.rearrange("(p j) c -> p j c", j=PACK)
+        w3_rows = w3.rearrange("(a p j) c -> a p j c", p=P, j=PACK)
+
+        load_scale_rows(nc.sync, tab_s, tab_scales)
+        load_scale_rows(nc.gpsimd, w2_s, w2_scales)
+        nc.sync.dma_start(idx[:], offs)
+        nc.sync.dma_start(p2[:], pos2)
+        nc.sync.dma_start(p1[:], pos1)
+        nc.sync.dma_start(out=w1_raw[0][:], in_=w1_rows[:, :, 0:PASS])
+        nc.sync.dma_start(out=w2_w[:].bitcast(I32), in_=w2_words[0].bitcast(I32))
+        nc.sync.dma_start(out=bias_c[:], in_=bias.rearrange("(b p t) -> p b t", p=P, t=PACK))
+        nc.sync.dma_start(
+            out=tab_w[:].bitcast(I32), in_=tab_words[0].rearrange("p t i -> p (t i)").bitcast(I32)
+        )
+        nc.sync.dma_start(out=unit_c[:], in_=unit.rearrange("(b p t) -> p b t", p=P, t=PACK))
+        nc.sync.dma_start(out=w1_raw[1][:], in_=w1_rows[:, :, PASS:H])
+        for b in range(GROUPS):
+            for a in range(GROUPS):
+                nc.sync.dma_start(out=w3_raw[a][b][:], in_=w3_rows[a, :, :, b * PASS : (b + 1) * PASS])
+        nc.sync.dma_start(out=gain_c[:], in_=gain.rearrange("(b p t) -> p b t", p=P, t=PACK))
+        nc.sync.dma_start(p3[:], pos3)
+
+        w2_codes = keep.tile([P, 2 * H], U8, name="w2_codes", align_bytes=64)
+        w2_plane = keep.tile([P, H], U8, name="w2_plane", align_bytes=64)
+        v_s = keep.tile([P, S], U8, name="v_s", align_bytes=64)
+        nc.vector.tensor_copy(v_s[:], tab_s[:].indirect(idx[:]))
+        nc.vector.tensor_copy(
+            out=w2_codes[:].rearrange("p (b t m e) -> p b m t e", b=GROUPS, t=PACK, e=2),
+            in_=w2_w[:].rearrange("p (b m t e) -> p b m t e", b=GROUPS, t=PACK, e=2),
+        )
+
+        nc.vector.tensor_copy(
+            out=w2_plane[:].rearrange("p (b t m) -> p b m t", b=GROUPS, t=PACK),
+            in_=w2_s[:].rearrange("p (b m t) -> p b m t", b=GROUPS, t=PACK),
+        )
+
+        v_w = []
+        for half in range(S // BANK):
+            words = keep.tile([P, BANK], U32, name="v_w%d" % half, align_bytes=64)
+            cols = BANK // LIST_ROWS
+            nc.vector.tensor_copy(words[:], tab_w[:].indirect(idx[:, half * cols : (half + 1) * cols]))
+            v_w.append(words)
+
+        w1_q, w3_q = {}, {}
+
+        def quantise_w1(b, pair):
+            grouped = ring.tile([P, 2 * PASS], BF16, name="w1_grouped", align_bytes=64)
+            codes = keep.tile([P, 2 * P], U32, name="w1_codes%d%d" % (b, pair), align_bytes=64)
+            plane = keep.tile([P, 2 * P], U8, name="w1_plane%d%d" % (b, pair), align_bytes=64)
+            round_and_deal(nc, grouped[:], w1_raw[b], pair)
+            nc.vector.quantize_mx(out=codes[:].bitcast(FP8X4), scales=plane[:], in_=grouped[:])
+            w1_q[b, pair] = (codes, plane)
+
+        def quantise_w3(b, pair):
+            grouped = ring.tile([P, GROUPS * 2 * PASS], BF16, name="w3_grouped", align_bytes=64)
+            codes = keep.tile([P, GROUPS * 2 * P], U32, name="w3_codes%d%d" % (b, pair), align_bytes=64)
+            plane = keep.tile([P, GROUPS * 2 * P], U8, name="w3_plane%d%d" % (b, pair), align_bytes=64)
+            for a in range(GROUPS):
+                round_and_deal(nc, grouped[:, a * 2 * PASS : (a + 1) * 2 * PASS], w3_raw[a][b], pair)
+            nc.vector.quantize_mx(out=codes[:].bitcast(FP8X4), scales=plane[:], in_=grouped[:])
+            w3_q[b, pair] = (codes, plane)
+
+        h = [keep.tile([P, S], F32, name="h%d" % i) for i in range(TILES)]
+        z_rows = [keep.tile([P, PACK, PAIRS], BF16, name="z_rows%d" % b) for b in range(GROUPS)]
+        z_q = []
+
+        def first_stage(i):
+            b, t = divmod(i, PACK)
+            codes, plane = w1_q[b, t // 2]
+            cols = slice((t % 2) * P, (t % 2 + 1) * P)
+            size = ring.tile([P, S], F32, name="size", bufs=3)
+            for half in range(S // BANK):
+                js = slice(half * BANK, (half + 1) * BANK)
+                first = psum.tile([P, BANK], F32, name="first")
+                second = psum.tile([P, BANK], F32, name="second")
+                nc.tensor.matmul_mx(
+                    out=first[:], lhsT=codes[:, cols].bitcast(FP8X4), lhsT_scale=plane[:, cols],
+                    rhs=v_w[half][:].bitcast(FP8X4), rhs_scale=v_s[:, js], start=True, stop=True,
+                )
+                nc.tensor.matmul_mx(
+                    out=second[:], lhsT=w2_codes[:, 2 * i * P : 2 * (i + 1) * P].bitcast(FP4X4),
+                    lhsT_scale=w2_plane[:, i * P : (i + 1) * P],
+                    rhs=v_w[half][:].bitcast(FP8X4), rhs_scale=v_s[:, js], start=True, stop=True,
+                )
+                nc.scalar.activation(out=size[:, js], in_=first[:], func=ACT.Abs)
+                nc.vector.scalar_tensor_tensor(
+                    out=h[i][:, js], in0=second[:], scalar=bias_c[:, b, t : t + 1], in1=size[:, js],
+                    op0=ALU.add, op1=ALU.add,
+                )
+
+        def pair_up(i, pieces):
+            b, t = divmod(i, PACK)
+            width = PAIRS // pieces
+            cols = width // LIST_ROWS
+            for u in range(pieces):
+                outer = ring.tile([P, width], F32, name="outer")
+                diff = ring.tile([P, width], F32, name="diff")
+                square = ring.tile([P, width], F32, name="square")
+                nc.vector.tensor_copy(outer[:], h[i][:].indirect(p2[:, u * cols : (u + 1) * cols]))
+                nc.vector.tensor_tensor(
+                    diff[:], h[i][:].indirect(p1[:, u * cols : (u + 1) * cols]), outer[:], ALU.subtract
+                )
+                nc.scalar.activation(out=square[:], in_=diff[:], func=ACT.Square)
+                nc.scalar.activation(
+                    out=z_rows[b][:, t, u * width : (u + 1) * width], in_=square[:], func=ACT.Sqrt,
+                    bias=unit_c[:, b, t : t + 1],
+                )
+
+        def quantise_z(b, weave, pieces):
+            grouped = keep.tile([P, PAIRS * PACK], BF16, name="z_grouped%d" % b, align_bytes=64)
+            codes = keep.tile([P, PAIRS], U32, name="z_codes%d" % b, align_bytes=64)
+            plane = keep.tile([P, PAIRS], U8, name="z_plane%d" % b, align_bytes=64)
+            width = PAIRS // pieces
+            for u in range(pieces):
+                ms = slice(u * width, (u + 1) * width)
+                part = grouped[:, u * width * PACK : (u + 1) * width * PACK]
+                weave(
+                    out=part.rearrange("p (c i t) -> p c t i", i=4, t=PACK),
+                    in_=z_rows[b][:, :, ms].rearrange("p t (c i) -> p c t i", i=4),
+                )
+                nc.vector.quantize_mx(out=codes[:, ms].bitcast(FP8X4), scales=plane[:, ms], in_=part)
+            z_q.append((codes, plane))
+
+        quantise_w1(0, 0)
+        quantise_w1(0, 1)
+        for i in range(TILES + 1):
+            if i < TILES:
+                first_stage(i)
+            if i == 1:
+                quantise_w1(1, 0)
+            if i == 3:
+                quantise_w1(1, 1)
+            if i >= 1:
+                pair_up(i - 1, 2 if i == TILES else 1)
+            if i == PACK + 1:
+                quantise_z(0, nc.scalar.copy, 1)
+            if i == PACK + 2:
+                quantise_w3(0, 0)
+        quantise_z(1, nc.vector.tensor_copy, 2)
+
+        out_rows = out.rearrange("(b p t) j -> b t p j", p=P, t=PACK)
+        SLICES = ((0, 384), (384, 768), (768, S))
+        scores, picked = {}, {}
+
+        def second_stage(i):
+            b, t = divmod(i, PACK)
+            codes, plane = w3_q[b, t // 2]
+            acc = psum.tile([P, BANK], F32, name="first")
+            for a in range(GROUPS):
+                cols = slice((2 * a + t % 2) * P, (2 * a + t % 2 + 1) * P)
+                nc.tensor.matmul_mx(
+                    out=acc[:], lhsT=codes[:, cols].bitcast(FP8X4), lhsT_scale=plane[:, cols],
+                    rhs=z_q[a][0][:].bitcast(FP8X4), rhs_scale=z_q[a][1][:],
+                    start=(a == 0), stop=(a == GROUPS - 1),
+                )
+            scores[i] = ring.tile([P, PAIRS], F32, name="scores", bufs=3)
+            nc.scalar.copy(out=scores[i][:], in_=acc[:])
+            picked[i] = ring.tile([P, S], F32, name="picked")
+
+        def pick(i, lo, hi):
+            nc.vector.tensor_copy(
+                picked[i][:, lo:hi], scores[i][:].indirect(p3[:, lo // LIST_ROWS : hi // LIST_ROWS])
+            )
+
+        def cap_and_store(i, lo, hi):
+            b, t = divmod(i, PACK)
+            result = ring.tile([P, hi - lo], F32, name="result", bufs=4)
+            nc.vector.scalar_tensor_tensor(
+                out=result[:], in0=h[i][:, lo:hi], scalar=gain_c[:, b, t : t + 1], in1=picked[i][:, lo:hi],
+                op0=ALU.mult, op1=ALU.min,
+            )
+            nc.sync.dma_start(out=out_rows[b, t, :, lo:hi], in_=result[:])
+
+        for i in range(TILES):
+            second_stage(i)
+            if i % 2 == 0 and i + 2 < TILES:
+                quantise_w3((i + 2) // PACK, (i + 2) % PACK // 2)
+            pick(i, *SLICES[0])
+            if i >= 1:
+                cap_and_store(i - 1, 0, S)
+            pick(i, *SLICES[1])
+            if i == TILES - 1:
+                cap_and_store(i, *SLICES[0])
+            pick(i, *SLICES[2])
+        cap_and_store(TILES - 1, *SLICES[1])
+        cap_and_store(TILES - 1, *SLICES[2])

@@ -25,9 +25,9 @@ TILES = H // P
 LIST_ROWS = 16
 
 
-def load_scale_rows(queue, plane, scales):
+def load_scale_rows(nc, plane, scales):
     for q in range(4):
-        queue.dma_start(
+        nc.sync.dma_start(
             out=plane[32 * q : 32 * q + 4, :].bitcast(I32),
             in_=scales[0, 4 * q : 4 * q + 4, :].bitcast(I32),
         )
@@ -35,7 +35,7 @@ def load_scale_rows(queue, plane, scales):
 
 def round_and_deal(nc, grouped, raw, pair):
     nc.scalar.copy(
-        out=grouped.rearrange("p (t m j) -> p m j t", t=2, j=PACK),
+        out=grouped.rearrange("p t (m j) -> p m j t", j=PACK),
         in_=raw[:].rearrange("p j (m t) -> p m j t", t=PACK)[:, :, :, 2 * pair : 2 * pair + 2],
     )
 
@@ -74,8 +74,7 @@ def tile_list_raceway_noise_scores_kernel(
         w1_rows = w1.rearrange("(p j) c -> p j c", j=PACK)
         w3_rows = w3.rearrange("(a p j) c -> a p j c", p=P, j=PACK)
 
-        load_scale_rows(nc.sync, tab_s, tab_scales)
-        load_scale_rows(nc.gpsimd, w2_s, w2_scales)
+        load_scale_rows(nc, tab_s, tab_scales)
         nc.sync.dma_start(idx[:], offs)
         nc.sync.dma_start(p2[:], pos2)
         nc.sync.dma_start(p1[:], pos1)
@@ -85,6 +84,7 @@ def tile_list_raceway_noise_scores_kernel(
         nc.sync.dma_start(
             out=tab_w[:].bitcast(I32), in_=tab_words[0].rearrange("p t i -> p (t i)").bitcast(I32)
         )
+        load_scale_rows(nc, w2_s, w2_scales)
         nc.sync.dma_start(out=unit_c[:], in_=unit.rearrange("(b p t) -> p b t", p=P, t=PACK))
         nc.sync.dma_start(out=w1_raw[1][:], in_=w1_rows[:, :, PASS:H])
         for b in range(GROUPS):
@@ -102,40 +102,48 @@ def tile_list_raceway_noise_scores_kernel(
             in_=w2_w[:].rearrange("p (b m t e) -> p b m t e", b=GROUPS, t=PACK, e=2),
         )
 
-        nc.vector.tensor_copy(
-            out=w2_plane[:].rearrange("p (b t m) -> p b m t", b=GROUPS, t=PACK),
-            in_=w2_s[:].rearrange("p (b m t) -> p b m t", b=GROUPS, t=PACK),
-        )
-
         v_w = []
         for half in range(S // BANK):
             words = keep.tile([P, BANK], U32, name="v_w%d" % half, align_bytes=64)
             cols = BANK // LIST_ROWS
             nc.vector.tensor_copy(words[:], tab_w[:].indirect(idx[:, half * cols : (half + 1) * cols]))
             v_w.append(words)
+            if half == 0:
+                nc.vector.tensor_copy(
+                    out=w2_plane[:].rearrange("p (b t m) -> p b m t", b=GROUPS, t=PACK),
+                    in_=w2_s[:].rearrange("p (b m t) -> p b m t", b=GROUPS, t=PACK),
+                )
 
-        w1_q, w3_q = {}, {}
+        w1_q = {}
 
         def quantise_w1(b, pair):
-            grouped = ring.tile([P, 2 * PASS], BF16, name="w1_grouped", align_bytes=64)
+            grouped = ring.tile([P, 2, PASS], BF16, name="w1_grouped", align_bytes=64)
             codes = keep.tile([P, 2 * P], U32, name="w1_codes%d%d" % (b, pair), align_bytes=64)
             plane = keep.tile([P, 2 * P], U8, name="w1_plane%d%d" % (b, pair), align_bytes=64)
             round_and_deal(nc, grouped[:], w1_raw[b], pair)
-            nc.vector.quantize_mx(out=codes[:].bitcast(FP8X4), scales=plane[:], in_=grouped[:])
+            nc.vector.quantize_mx(out=codes[:].bitcast(FP8X4), scales=plane[:], in_=grouped[:].rearrange("p t c -> p (t c)"))
             w1_q[b, pair] = (codes, plane)
 
-        def quantise_w3(b, pair):
-            grouped = ring.tile([P, GROUPS * 2 * PASS], BF16, name="w3_grouped", align_bytes=64)
-            codes = keep.tile([P, GROUPS * 2 * P], U32, name="w3_codes%d%d" % (b, pair), align_bytes=64)
-            plane = keep.tile([P, GROUPS * 2 * P], U8, name="w3_plane%d%d" % (b, pair), align_bytes=64)
+        w3_codes = {}
+        w3_plane = [keep.tile([P, GROUPS * P], U8, name="w3_plane%d" % i, align_bytes=64) for i in range(TILES)]
+        w3_grouped = {}
+
+        def round_w3(b, pair):
+            grouped = ring.tile([P, 2, GROUPS, PASS], BF16, name="w3_grouped", align_bytes=64)
             for a in range(GROUPS):
-                round_and_deal(nc, grouped[:, a * 2 * PASS : (a + 1) * 2 * PASS], w3_raw[a][b], pair)
-            nc.vector.quantize_mx(out=codes[:].bitcast(FP8X4), scales=plane[:], in_=grouped[:])
-            w3_q[b, pair] = (codes, plane)
+                round_and_deal(nc, grouped[:, :, a, :], w3_raw[a][b], pair)
+            w3_grouped[b, pair] = grouped
+
+        def quantise_w3(i):
+            b, t = divmod(i, PACK)
+            w3_codes[i] = keep.tile([P, GROUPS * P], U32, name="w3_codes", tag="slot%d" % i, align_bytes=64)
+            nc.vector.quantize_mx(
+                out=w3_codes[i][:].bitcast(FP8X4), scales=w3_plane[i][:],
+                in_=w3_grouped[b, t // 2][:, t % 2, :, :].rearrange("p a c -> p (a c)"),
+            )
 
         h = [keep.tile([P, S], F32, name="h%d" % i) for i in range(TILES)]
         z_rows = [keep.tile([P, PACK, PAIRS], BF16, name="z_rows%d" % b) for b in range(GROUPS)]
-        z_q = []
 
         def first_stage(i):
             b, t = divmod(i, PACK)
@@ -166,12 +174,15 @@ def tile_list_raceway_noise_scores_kernel(
             width = PAIRS // pieces
             cols = width // LIST_ROWS
             for u in range(pieces):
-                outer = ring.tile([P, width], F32, name="outer")
+                if pieces == 1:
+                    outer = ring.tile([P, width], F32, name="outer")[:]
+                else:
+                    outer = keep.tile([P, width], F32, name="outer", tag="slot%d" % u, align_bytes=64)[:]
                 diff = ring.tile([P, width], F32, name="diff")
                 square = ring.tile([P, width], F32, name="square")
-                nc.vector.tensor_copy(outer[:], h[i][:].indirect(p2[:, u * cols : (u + 1) * cols]))
+                nc.vector.tensor_copy(outer, h[i][:].indirect(p2[:, u * cols : (u + 1) * cols]))
                 nc.vector.tensor_tensor(
-                    diff[:], h[i][:].indirect(p1[:, u * cols : (u + 1) * cols]), outer[:], ALU.subtract
+                    diff[:], h[i][:].indirect(p1[:, u * cols : (u + 1) * cols]), outer, ALU.subtract
                 )
                 nc.scalar.activation(out=square[:], in_=diff[:], func=ACT.Square)
                 nc.scalar.activation(
@@ -179,20 +190,24 @@ def tile_list_raceway_noise_scores_kernel(
                     bias=unit_c[:, b, t : t + 1],
                 )
 
-        def quantise_z(b, weave, pieces):
-            grouped = keep.tile([P, PAIRS * PACK], BF16, name="z_grouped%d" % b, align_bytes=64)
-            codes = keep.tile([P, PAIRS], U32, name="z_codes%d" % b, align_bytes=64)
-            plane = keep.tile([P, PAIRS], U8, name="z_plane%d" % b, align_bytes=64)
-            width = PAIRS // pieces
-            for u in range(pieces):
-                ms = slice(u * width, (u + 1) * width)
-                part = grouped[:, u * width * PACK : (u + 1) * width * PACK]
-                weave(
-                    out=part.rearrange("p (c i t) -> p c t i", i=4, t=PACK),
-                    in_=z_rows[b][:, :, ms].rearrange("p t (c i) -> p c t i", i=4),
-                )
-                nc.vector.quantize_mx(out=codes[:, ms].bitcast(FP8X4), scales=plane[:, ms], in_=part)
-            z_q.append((codes, plane))
+        z_grouped = [keep.tile([P, PAIRS, PACK], BF16, name="z_grouped%d" % a, align_bytes=64) for a in range(GROUPS)]
+        z_codes = [keep.tile([P, PAIRS], U32, name="z_codes%d" % a, align_bytes=64) for a in range(GROUPS)]
+        z_plane = [keep.tile([P, PAIRS], U8, name="z_plane%d" % a, align_bytes=64) for a in range(GROUPS)]
+
+        def weave_z(copy, a, ms):
+            copy(
+                out=z_grouped[a][:, ms, :].rearrange("p (c i) t -> p c t i", i=4),
+                in_=z_rows[a][:, :, ms].rearrange("p t (c i) -> p c t i", i=4),
+            )
+
+        def quantise_z(a, ms):
+            nc.vector.quantize_mx(
+                out=z_codes[a][:, ms].bitcast(FP8X4), scales=z_plane[a][:, ms],
+                in_=z_grouped[a][:, ms, :].rearrange("p m t -> p (m t)"),
+            )
+
+        whole = slice(0, PAIRS)
+        halves = (slice(0, PAIRS // 2), slice(PAIRS // 2, PAIRS))
 
         quantise_w1(0, 0)
         quantise_w1(0, 1)
@@ -206,28 +221,32 @@ def tile_list_raceway_noise_scores_kernel(
             if i >= 1:
                 pair_up(i - 1, 2 if i == TILES else 1)
             if i == PACK + 1:
-                quantise_z(0, nc.scalar.copy, 1)
+                weave_z(nc.scalar.copy, 0, whole)
+                quantise_z(0, whole)
             if i == PACK + 2:
-                quantise_w3(0, 0)
-        quantise_z(1, nc.vector.tensor_copy, 2)
+                round_w3(0, 0)
+        weave_z(nc.vector.tensor_copy, 1, halves[0])
+        quantise_w3(0)
+        weave_z(nc.vector.tensor_copy, 1, halves[1])
+        quantise_z(1, halves[0])
+        quantise_z(1, halves[1])
 
         out_rows = out.rearrange("(b p t) j -> b t p j", p=P, t=PACK)
         SLICES = ((0, 384), (384, 768), (768, S))
         scores, picked = {}, {}
 
-        def second_stage(i):
-            b, t = divmod(i, PACK)
-            codes, plane = w3_q[b, t // 2]
-            acc = psum.tile([P, BANK], F32, name="first")
-            for a in range(GROUPS):
-                cols = slice((2 * a + t % 2) * P, (2 * a + t % 2 + 1) * P)
-                nc.tensor.matmul_mx(
-                    out=acc[:], lhsT=codes[:, cols].bitcast(FP8X4), lhsT_scale=plane[:, cols],
-                    rhs=z_q[a][0][:].bitcast(FP8X4), rhs_scale=z_q[a][1][:],
-                    start=(a == 0), stop=(a == GROUPS - 1),
-                )
+        def second_stage(i, parts):
             scores[i] = ring.tile([P, PAIRS], F32, name="scores", bufs=3)
-            nc.scalar.copy(out=scores[i][:], in_=acc[:])
+            for ms in parts:
+                acc = psum.tile([P, ms.stop - ms.start], F32, name="first")
+                for a in range(GROUPS):
+                    cols = slice(a * P, (a + 1) * P)
+                    nc.tensor.matmul_mx(
+                        out=acc[:], lhsT=w3_codes[i][:, cols].bitcast(FP8X4), lhsT_scale=w3_plane[i][:, cols],
+                        rhs=z_codes[a][:, ms].bitcast(FP8X4), rhs_scale=z_plane[a][:, ms],
+                        start=(a == 0), stop=(a == GROUPS - 1),
+                    )
+                nc.scalar.copy(out=scores[i][:, ms], in_=acc[:])
             picked[i] = ring.tile([P, S], F32, name="picked")
 
         def pick(i, lo, hi):
@@ -245,9 +264,11 @@ def tile_list_raceway_noise_scores_kernel(
             nc.sync.dma_start(out=out_rows[b, t, :, lo:hi], in_=result[:])
 
         for i in range(TILES):
-            second_stage(i)
+            second_stage(i, halves if i == 0 else (whole,))
             if i % 2 == 0 and i + 2 < TILES:
-                quantise_w3((i + 2) // PACK, (i + 2) % PACK // 2)
+                round_w3((i + 2) // PACK, (i + 2) % PACK // 2)
+            if i + 1 < TILES:
+                quantise_w3(i + 1)
             pick(i, *SLICES[0])
             if i >= 1:
                 cap_and_store(i - 1, 0, S)

@@ -98,8 +98,8 @@ def tile_list_raceway_noise_scores_kernel(
         v_s = keep.tile([P, S], U8, name="v_s", align_bytes=64)
         nc.vector.tensor_copy(v_s[:], tab_s[:].indirect(idx[:]))
         nc.vector.tensor_copy(
-            out=w2_codes[:].rearrange("p (b t m e) -> p b m t e", b=GROUPS, t=PACK, e=2),
-            in_=w2_w[:].rearrange("p (b m t e) -> p b m t e", b=GROUPS, t=PACK, e=2),
+            out=w2_codes[:].rearrange("p (b t m e) -> p b t m e", b=GROUPS, t=PACK, e=2),
+            in_=w2_w[:].rearrange("p (b m t e) -> p b t m e", b=GROUPS, t=PACK, e=2),
         )
 
         v_w = []
@@ -110,8 +110,8 @@ def tile_list_raceway_noise_scores_kernel(
             v_w.append(words)
             if half == 0:
                 nc.vector.tensor_copy(
-                    out=w2_plane[:].rearrange("p (b t m) -> p b m t", b=GROUPS, t=PACK),
-                    in_=w2_s[:].rearrange("p (b m t) -> p b m t", b=GROUPS, t=PACK),
+                    out=w2_plane[:].rearrange("p (b t m) -> p b t m", b=GROUPS, t=PACK),
+                    in_=w2_s[:].rearrange("p (b m t) -> p b t m", b=GROUPS, t=PACK),
                 )
 
         w1_q = {}
@@ -145,11 +145,14 @@ def tile_list_raceway_noise_scores_kernel(
         h = [keep.tile([P, S], F32, name="h%d" % i) for i in range(TILES)]
         z_rows = [keep.tile([P, PACK, PAIRS], BF16, name="z_rows%d" % b) for b in range(GROUPS)]
 
+        sizes = {}
+
         def first_stage(i):
             b, t = divmod(i, PACK)
             codes, plane = w1_q[b, t // 2]
             cols = slice((t % 2) * P, (t % 2 + 1) * P)
-            size = ring.tile([P, S], F32, name="size", bufs=3)
+            size = ring.tile([P, S], F32, name="size", bufs=4)
+            sizes[i] = size
             for half in range(S // BANK):
                 js = slice(half * BANK, (half + 1) * BANK)
                 first = psum.tile([P, BANK], F32, name="first")
@@ -175,16 +178,20 @@ def tile_list_raceway_noise_scores_kernel(
             cols = width // LIST_ROWS
             for u in range(pieces):
                 if pieces == 1:
-                    outer = ring.tile([P, width], F32, name="outer")[:]
+                    outer = sizes[i + 1][:, 0:PAIRS]
+                    diff = sizes[i + 1][:, PAIRS:S]
                 else:
+                    diff = ring.tile([P, width], F32, name="diff")[:]
                     outer = keep.tile([P, width], F32, name="outer", tag="slot%d" % u, align_bytes=64)[:]
-                diff = ring.tile([P, width], F32, name="diff")
                 square = ring.tile([P, width], F32, name="square")
                 nc.vector.tensor_copy(outer, h[i][:].indirect(p2[:, u * cols : (u + 1) * cols]))
                 nc.vector.tensor_tensor(
-                    diff[:], h[i][:].indirect(p1[:, u * cols : (u + 1) * cols]), outer, ALU.subtract
+                    diff, h[i][:].indirect(p1[:, u * cols : (u + 1) * cols]), outer, ALU.subtract
                 )
-                nc.scalar.activation(out=square[:], in_=diff[:], func=ACT.Square)
+                if pieces == 1:
+                    nc.gpsimd.tensor_tensor(square[:], diff, diff, ALU.mult)
+                else:
+                    nc.scalar.activation(out=square[:], in_=diff, func=ACT.Square)
                 nc.scalar.activation(
                     out=z_rows[b][:, t, u * width : (u + 1) * width], in_=square[:], func=ACT.Sqrt,
                     bias=unit_c[:, b, t : t + 1],

@@ -18,11 +18,11 @@ ACT = mybir.ActivationFunctionType
 
 P = 128
 PACK = 4
-PASS = P * PACK
+GROUP = P * PACK
 BANK = 512
-GROUPS = H // PASS
+GROUPS = H // GROUP
 TILES = H // P
-LIST_ROWS = 16
+PER_COLUMN = 16
 
 
 def load_scale_rows(nc, plane, scales):
@@ -40,6 +40,10 @@ def round_and_deal(nc, grouped, raw, pair):
     )
 
 
+def entries(listed, lo, hi):
+    return listed[:, lo // PER_COLUMN : hi // PER_COLUMN]
+
+
 def tile_list_raceway_noise_scores_kernel(
     tc, tab_words, tab_scales, offs, pos1, pos2, pos3, w1, w2_words, w2_scales, bias, unit, w3, gain, out
 ):
@@ -49,17 +53,20 @@ def tile_list_raceway_noise_scores_kernel(
         ring = ctx.enter_context(tc.tile_pool(name="ring", bufs=2))
         psum = ctx.enter_context(tc.psum_pool(name="psum", bufs=4))
 
-        idx = keep.tile([P, S // LIST_ROWS], U16, name="idx")
-        p1 = keep.tile([P, PAIRS // LIST_ROWS], U16, name="p1")
-        p2 = keep.tile([P, PAIRS // LIST_ROWS], U16, name="p2")
-        p3 = keep.tile([P, S // LIST_ROWS], U16, name="p3")
+        idx = keep.tile([P, S // PER_COLUMN], U16, name="idx")
+        p1 = keep.tile([P, PAIRS // PER_COLUMN], U16, name="p1")
+        p2 = keep.tile([P, PAIRS // PER_COLUMN], U16, name="p2")
+        p3 = keep.tile([P, S // PER_COLUMN], U16, name="p3")
         tab_w = keep.tile([P, T], U32, name="tab_w", align_bytes=64)
         tab_s = keep.tile([P, T], U8, name="tab_s", align_bytes=64)
         w2_w = keep.tile([P, 2 * H], U8, name="w2_w", align_bytes=64)
         w2_s = keep.tile([P, H], U8, name="w2_s", align_bytes=64)
-        w1_raw = [keep.tile([P, PACK, PASS], F32, name="w1_raw%d" % b) for b in range(GROUPS)]
+        w1_raw = [
+            [keep.tile([P, PACK, GROUP // 2], F32, name="w1_raw0%d" % u) for u in range(2)],
+            [keep.tile([P, PACK, GROUP], F32, name="w1_raw1")],
+        ]
         w3_raw = [
-            [keep.tile([P, PACK, PASS], F32, name="w3_raw%d%d" % (a, b)) for b in range(GROUPS)]
+            [keep.tile([P, PACK, GROUP], F32, name="w3_raw%d%d" % (a, b)) for b in range(GROUPS)]
             for a in range(GROUPS)
         ]
         bias_c = keep.tile([P, GROUPS, PACK], F32, name="bias_c")
@@ -78,18 +85,19 @@ def tile_list_raceway_noise_scores_kernel(
         nc.sync.dma_start(idx[:], offs)
         nc.sync.dma_start(p2[:], pos2)
         nc.sync.dma_start(p1[:], pos1)
-        nc.sync.dma_start(out=w1_raw[0][:], in_=w1_rows[:, :, 0:PASS])
+        nc.sync.dma_start(out=w1_raw[0][0][:], in_=w1_rows[:, :, 0 : GROUP // 2])
         nc.sync.dma_start(out=w2_w[:].bitcast(I32), in_=w2_words[0].bitcast(I32))
         nc.sync.dma_start(out=bias_c[:], in_=bias.rearrange("(b p t) -> p b t", p=P, t=PACK))
         nc.sync.dma_start(
             out=tab_w[:].bitcast(I32), in_=tab_words[0].rearrange("p t i -> p (t i)").bitcast(I32)
         )
+        nc.sync.dma_start(out=w1_raw[0][1][:], in_=w1_rows[:, :, GROUP // 2 : GROUP])
         load_scale_rows(nc, w2_s, w2_scales)
         nc.sync.dma_start(out=unit_c[:], in_=unit.rearrange("(b p t) -> p b t", p=P, t=PACK))
-        nc.sync.dma_start(out=w1_raw[1][:], in_=w1_rows[:, :, PASS:H])
+        nc.sync.dma_start(out=w1_raw[1][0][:], in_=w1_rows[:, :, GROUP:H])
         for b in range(GROUPS):
             for a in range(GROUPS):
-                nc.sync.dma_start(out=w3_raw[a][b][:], in_=w3_rows[a, :, :, b * PASS : (b + 1) * PASS])
+                nc.sync.dma_start(out=w3_raw[a][b][:], in_=w3_rows[a, :, :, b * GROUP : (b + 1) * GROUP])
         nc.sync.dma_start(out=gain_c[:], in_=gain.rearrange("(b p t) -> p b t", p=P, t=PACK))
         nc.sync.dma_start(p3[:], pos3)
 
@@ -101,101 +109,97 @@ def tile_list_raceway_noise_scores_kernel(
             out=w2_codes[:].rearrange("p (b t m e) -> p b t m e", b=GROUPS, t=PACK, e=2),
             in_=w2_w[:].rearrange("p (b m t e) -> p b t m e", b=GROUPS, t=PACK, e=2),
         )
-
-        v_w = []
-        for half in range(S // BANK):
-            words = keep.tile([P, BANK], U32, name="v_w%d" % half, align_bytes=64)
-            cols = BANK // LIST_ROWS
-            nc.vector.tensor_copy(words[:], tab_w[:].indirect(idx[:, half * cols : (half + 1) * cols]))
-            v_w.append(words)
-            if half == 0:
-                nc.vector.tensor_copy(
-                    out=w2_plane[:].rearrange("p (b t m) -> p b t m", b=GROUPS, t=PACK),
-                    in_=w2_s[:].rearrange("p (b m t) -> p b t m", b=GROUPS, t=PACK),
-                )
+        v_w = [keep.tile([P, BANK], U32, name="v_w%d" % half, align_bytes=64) for half in range(S // BANK)]
+        nc.vector.tensor_copy(v_w[0][:], tab_w[:].indirect(entries(idx, 0, BANK)))
+        nc.vector.tensor_copy(
+            out=w2_plane[:].rearrange("p (b t m) -> p b t m", b=GROUPS, t=PACK),
+            in_=w2_s[:].rearrange("p (b m t) -> p b t m", b=GROUPS, t=PACK),
+        )
+        nc.vector.tensor_copy(v_w[1][:], tab_w[:].indirect(entries(idx, BANK, S)))
 
         w1_q = {}
 
         def quantise_w1(b, pair):
-            grouped = ring.tile([P, 2, PASS], BF16, name="w1_grouped", align_bytes=64)
+            grouped = ring.tile([P, 2, GROUP], BF16, name="w1_grouped", align_bytes=64)
             codes = keep.tile([P, 2 * P], U32, name="w1_codes%d%d" % (b, pair), align_bytes=64)
             plane = keep.tile([P, 2 * P], U8, name="w1_plane%d%d" % (b, pair), align_bytes=64)
-            round_and_deal(nc, grouped[:], w1_raw[b], pair)
-            nc.vector.quantize_mx(out=codes[:].bitcast(FP8X4), scales=plane[:], in_=grouped[:].rearrange("p t c -> p (t c)"))
+            width = GROUP // len(w1_raw[b])
+            for u, raw in enumerate(w1_raw[b]):
+                round_and_deal(nc, grouped[:, :, u * width : (u + 1) * width], raw, pair)
+            nc.vector.quantize_mx(
+                out=codes[:].bitcast(FP8X4), scales=plane[:], in_=grouped[:].rearrange("p t c -> p (t c)")
+            )
             w1_q[b, pair] = (codes, plane)
 
-        w3_codes = {}
-        w3_plane = [keep.tile([P, GROUPS * P], U8, name="w3_plane%d" % i, align_bytes=64) for i in range(TILES)]
+        w3_grouped_tag = {(0, 0): "w3_first", (0, 1): "last_diff", (1, 0): "late0", (1, 1): "late1"}
+        w3_q = {}
         w3_grouped = {}
 
         def round_w3(b, pair):
-            grouped = ring.tile([P, 2, GROUPS, PASS], BF16, name="w3_grouped", align_bytes=64)
+            grouped = keep.tile(
+                [P, 2, GROUPS, GROUP], BF16, name="w3_grouped", tag=w3_grouped_tag[b, pair], align_bytes=64
+            )
             for a in range(GROUPS):
                 round_and_deal(nc, grouped[:, :, a, :], w3_raw[a][b], pair)
             w3_grouped[b, pair] = grouped
 
-        def quantise_w3(i):
+        def quantise_w3(i, count):
             b, t = divmod(i, PACK)
-            w3_codes[i] = keep.tile([P, GROUPS * P], U32, name="w3_codes", tag="slot%d" % i, align_bytes=64)
+            width = GROUPS * P
+            tag = ("late%d" if count == 1 else "w3_codes%d") % i
+            codes = keep.tile([P, count * width], U32, name="w3_codes", tag=tag, align_bytes=64)
+            plane = keep.tile([P, count * width], U8, name="w3_plane%d" % i, align_bytes=64)
             nc.vector.quantize_mx(
-                out=w3_codes[i][:].bitcast(FP8X4), scales=w3_plane[i][:],
-                in_=w3_grouped[b, t // 2][:, t % 2, :, :].rearrange("p a c -> p (a c)"),
+                out=codes[:].bitcast(FP8X4), scales=plane[:],
+                in_=w3_grouped[b, t // 2][:, t % 2 : t % 2 + count, :, :].rearrange("p t a c -> p (t a c)"),
             )
+            for u in range(count):
+                w3_q[i + u] = (codes, plane, u * width)
 
         h = [keep.tile([P, S], F32, name="h%d" % i) for i in range(TILES)]
         z_rows = [keep.tile([P, PACK, PAIRS], BF16, name="z_rows%d" % b) for b in range(GROUPS)]
 
-        sizes = {}
+        sizes, signed = {}, {}
 
-        def first_stage(i):
+        def products(i):
             b, t = divmod(i, PACK)
             codes, plane = w1_q[b, t // 2]
             cols = slice((t % 2) * P, (t % 2 + 1) * P)
-            size = ring.tile([P, S], F32, name="size", bufs=4)
-            sizes[i] = size
+            sizes[i] = ring.tile([P, S], F32, name="size", bufs=4)
             for half in range(S // BANK):
                 js = slice(half * BANK, (half + 1) * BANK)
-                first = psum.tile([P, BANK], F32, name="first")
-                second = psum.tile([P, BANK], F32, name="second")
+                for_scalar = psum.tile([P, BANK], F32, name="for_scalar")
+                signed[i, half] = psum.tile([P, BANK], F32, name="for_vector")
                 nc.tensor.matmul_mx(
-                    out=first[:], lhsT=codes[:, cols].bitcast(FP8X4), lhsT_scale=plane[:, cols],
+                    out=for_scalar[:], lhsT=codes[:, cols].bitcast(FP8X4), lhsT_scale=plane[:, cols],
                     rhs=v_w[half][:].bitcast(FP8X4), rhs_scale=v_s[:, js], start=True, stop=True,
                 )
                 nc.tensor.matmul_mx(
-                    out=second[:], lhsT=w2_codes[:, 2 * i * P : 2 * (i + 1) * P].bitcast(FP4X4),
+                    out=signed[i, half][:], lhsT=w2_codes[:, 2 * i * P : 2 * (i + 1) * P].bitcast(FP4X4),
                     lhsT_scale=w2_plane[:, i * P : (i + 1) * P],
                     rhs=v_w[half][:].bitcast(FP8X4), rhs_scale=v_s[:, js], start=True, stop=True,
                 )
-                nc.scalar.activation(out=size[:, js], in_=first[:], func=ACT.Abs)
-                nc.vector.scalar_tensor_tensor(
-                    out=h[i][:, js], in0=second[:], scalar=bias_c[:, b, t : t + 1], in1=size[:, js],
-                    op0=ALU.add, op1=ALU.add,
-                )
+                nc.scalar.activation(out=sizes[i][:, js], in_=for_scalar[:], func=ACT.Abs)
 
-        def pair_up(i, pieces):
+        def add_up(i, half):
             b, t = divmod(i, PACK)
-            width = PAIRS // pieces
-            cols = width // LIST_ROWS
-            for u in range(pieces):
-                if pieces == 1:
-                    outer = sizes[i + 1][:, 0:PAIRS]
-                    diff = sizes[i + 1][:, PAIRS:S]
-                else:
-                    diff = ring.tile([P, width], F32, name="diff")[:]
-                    outer = keep.tile([P, width], F32, name="outer", tag="slot%d" % u, align_bytes=64)[:]
-                square = ring.tile([P, width], F32, name="square")
-                nc.vector.tensor_copy(outer, h[i][:].indirect(p2[:, u * cols : (u + 1) * cols]))
-                nc.vector.tensor_tensor(
-                    diff, h[i][:].indirect(p1[:, u * cols : (u + 1) * cols]), outer, ALU.subtract
-                )
-                if pieces == 1:
-                    nc.gpsimd.tensor_tensor(square[:], diff, diff, ALU.mult)
-                else:
-                    nc.scalar.activation(out=square[:], in_=diff, func=ACT.Square)
-                nc.scalar.activation(
-                    out=z_rows[b][:, t, u * width : (u + 1) * width], in_=square[:], func=ACT.Sqrt,
-                    bias=unit_c[:, b, t : t + 1],
-                )
+            js = slice(half * BANK, (half + 1) * BANK)
+            nc.vector.scalar_tensor_tensor(
+                out=h[i][:, js], in0=signed[i, half][:], scalar=bias_c[:, b, t : t + 1], in1=sizes[i][:, js],
+                op0=ALU.add, op1=ALU.add,
+            )
+
+        def pick_outer(i, outer, ms):
+            nc.vector.tensor_copy(outer, h[i][:].indirect(entries(p2, ms.start, ms.stop)))
+
+        def distance(i, outer, diff, ms):
+            b, t = divmod(i, PACK)
+            square = ring.tile([P, ms.stop - ms.start], F32, name="square")
+            nc.vector.tensor_tensor(diff, h[i][:].indirect(entries(p1, ms.start, ms.stop)), outer, ALU.subtract)
+            nc.scalar.activation(out=square[:], in_=diff, func=ACT.Square)
+            nc.scalar.activation(
+                out=z_rows[b][:, t, ms], in_=square[:], func=ACT.Sqrt, bias=unit_c[:, b, t : t + 1]
+            )
 
         z_grouped = [keep.tile([P, PAIRS, PACK], BF16, name="z_grouped%d" % a, align_bytes=64) for a in range(GROUPS)]
         z_codes = [keep.tile([P, PAIRS], U32, name="z_codes%d" % a, align_bytes=64) for a in range(GROUPS)]
@@ -213,53 +217,66 @@ def tile_list_raceway_noise_scores_kernel(
                 in_=z_grouped[a][:, ms, :].rearrange("p m t -> p (m t)"),
             )
 
-        whole = slice(0, PAIRS)
-        halves = (slice(0, PAIRS // 2), slice(PAIRS // 2, PAIRS))
+        all_pairs = slice(0, PAIRS)
+        half_pairs = (slice(0, PAIRS // 2), slice(PAIRS // 2, PAIRS))
 
         quantise_w1(0, 0)
         quantise_w1(0, 1)
-        for i in range(TILES + 1):
-            if i < TILES:
-                first_stage(i)
-            if i == 1:
-                quantise_w1(1, 0)
-            if i == 3:
-                quantise_w1(1, 1)
-            if i >= 1:
-                pair_up(i - 1, 2 if i == TILES else 1)
-            if i == PACK + 1:
-                weave_z(nc.scalar.copy, 0, whole)
-                quantise_z(0, whole)
-            if i == PACK + 2:
+        products(0)
+        products(1)
+        add_up(0, 0)
+        add_up(0, 1)
+        for i in range(TILES - 1):
+            if i + 2 < TILES:
+                products(i + 2)
+            outer, diff = sizes[i + 1][:, 0:PAIRS], sizes[i + 1][:, PAIRS:S]
+            add_up(i + 1, 0)
+            pick_outer(i, outer, all_pairs)
+            add_up(i + 1, 1)
+            distance(i, outer, diff, all_pairs)
+            if i in (0, 2):
+                quantise_w1(1, i // 2)
+            if i == PACK - 1:
                 round_w3(0, 0)
-        weave_z(nc.vector.tensor_copy, 1, halves[0])
-        quantise_w3(0)
-        weave_z(nc.vector.tensor_copy, 1, halves[1])
-        quantise_z(1, halves[0])
-        quantise_z(1, halves[1])
+            if i + 2 == TILES - 1:
+                weave_z(nc.scalar.copy, 0, all_pairs)
+                quantise_z(0, all_pairs)
+        for u, ms in enumerate(half_pairs):
+            outer = keep.tile([P, PAIRS // 2], F32, name="outer", tag="late%d" % u, align_bytes=64)
+            diff = keep.tile([P, PAIRS // 2], F32, name="diff", tag=("diff", "last_diff")[u], align_bytes=64)
+            pick_outer(TILES - 1, outer[:], ms)
+            distance(TILES - 1, outer[:], diff[:], ms)
+        weave_z(nc.vector.tensor_copy, 1, half_pairs[0])
+        quantise_w3(0, 1)
+        weave_z(nc.vector.tensor_copy, 1, half_pairs[1])
+        quantise_z(1, half_pairs[0])
+        quantise_z(1, half_pairs[1])
 
         out_rows = out.rearrange("(b p t) j -> b t p j", p=P, t=PACK)
-        SLICES = ((0, 384), (384, 768), (768, S))
-        scores, picked = {}, {}
+        quarters = tuple((u * S // 4, (u + 1) * S // 4) for u in range(4))
+        halves = ((0, S // 2), (S // 2, S))
+        taper = halves[:1] + quarters[2:]
+        scores = keep.tile([P, TILES * PAIRS], F32, name="scores")
+        picked = {}
 
-        def second_stage(i, parts):
-            scores[i] = ring.tile([P, PAIRS], F32, name="scores", bufs=3)
+        def second_product(i, parts):
+            codes, plane, start = w3_q[i]
+            at = (TILES - 1 - i) * PAIRS
             for ms in parts:
-                acc = psum.tile([P, ms.stop - ms.start], F32, name="first")
+                acc = psum.tile([P, ms.stop - ms.start], F32, name="for_scalar")
                 for a in range(GROUPS):
-                    cols = slice(a * P, (a + 1) * P)
+                    cols = slice(start + a * P, start + (a + 1) * P)
                     nc.tensor.matmul_mx(
-                        out=acc[:], lhsT=w3_codes[i][:, cols].bitcast(FP8X4), lhsT_scale=w3_plane[i][:, cols],
+                        out=acc[:], lhsT=codes[:, cols].bitcast(FP8X4), lhsT_scale=plane[:, cols],
                         rhs=z_codes[a][:, ms].bitcast(FP8X4), rhs_scale=z_plane[a][:, ms],
                         start=(a == 0), stop=(a == GROUPS - 1),
                     )
-                nc.scalar.copy(out=scores[i][:, ms], in_=acc[:])
-            picked[i] = ring.tile([P, S], F32, name="picked")
+                nc.scalar.copy(out=scores[:, at + ms.start : at + ms.stop], in_=acc[:])
 
         def pick(i, lo, hi):
-            nc.vector.tensor_copy(
-                picked[i][:, lo:hi], scores[i][:].indirect(p3[:, lo // LIST_ROWS : hi // LIST_ROWS])
-            )
+            at = (TILES - 1 - i) * PAIRS
+            window = scores[:, at : min(at + 2 * PAIRS, TILES * PAIRS)]
+            nc.vector.tensor_copy(picked[i][:, lo:hi], window.indirect(entries(p3, lo, hi)))
 
         def cap_and_store(i, lo, hi):
             b, t = divmod(i, PACK)
@@ -270,18 +287,26 @@ def tile_list_raceway_noise_scores_kernel(
             )
             nc.sync.dma_start(out=out_rows[b, t, :, lo:hi], in_=result[:])
 
+        second_product(0, half_pairs)
+        quantise_w3(1, 1)
+        second_product(1, (all_pairs,))
+        round_w3(0, 1)
         for i in range(TILES):
-            second_stage(i, halves if i == 0 else (whole,))
-            if i % 2 == 0 and i + 2 < TILES:
-                round_w3((i + 2) // PACK, (i + 2) % PACK // 2)
-            if i + 1 < TILES:
-                quantise_w3(i + 1)
-            pick(i, *SLICES[0])
+            slices = quarters if i == 0 else taper if i == TILES - 1 else halves
+            picked[i] = ring.tile([P, S], F32, name="picked")
+            pick(i, *slices[0])
             if i >= 1:
                 cap_and_store(i - 1, 0, S)
-            pick(i, *SLICES[1])
+            if i + 2 < TILES:
+                if i % 2 == 0:
+                    quantise_w3(i + 2, 2)
+                second_product(i + 2, (all_pairs,))
+            if i < 2:
+                round_w3(1, i)
+            pick(i, *slices[1])
             if i == TILES - 1:
-                cap_and_store(i, *SLICES[0])
-            pick(i, *SLICES[2])
-        cap_and_store(TILES - 1, *SLICES[1])
-        cap_and_store(TILES - 1, *SLICES[2])
+                cap_and_store(i, *slices[0])
+            for part in slices[2:]:
+                pick(i, *part)
+        for part in taper[1:]:
+            cap_and_store(TILES - 1, *part)

from contextlib import ExitStack

import concourse.mybir as mybir

K, T, S, PAIRS, H = 512, 4096, 1024, 512, 1024
FLOPS = 2 * (2 * K * H * S + H * H * PAIRS)

F32 = mybir.dt.float32
BF16 = mybir.dt.bfloat16
I32 = mybir.dt.int32
U32 = mybir.dt.uint32
U16 = mybir.dt.uint16
U8 = mybir.dt.uint8
FP8X4 = mybir.dt.float8_e4m3fn_x4
FP4X4 = mybir.dt.float4_e2m1fn_x4
ALU = mybir.AluOpType
ACT = mybir.ActivationFunctionType

P = 128
PACK = 4
GROUP = P * PACK
BANK = 512
GROUPS = H // GROUP
TILES = H // P
PER_COLUMN = 16


def load_scale_rows(nc, plane, scales):
    for q in range(4):
        nc.sync.dma_start(
            out=plane[32 * q : 32 * q + 4, :].bitcast(I32),
            in_=scales[0, 4 * q : 4 * q + 4, :].bitcast(I32),
        )


def round_and_deal(nc, grouped, raw, pair):
    nc.scalar.copy(
        out=grouped.rearrange("p t (m j) -> p m j t", j=PACK),
        in_=raw[:].rearrange("p j (m t) -> p m j t", t=PACK)[:, :, :, 2 * pair : 2 * pair + 2],
    )


def entries(listed, lo, hi):
    return listed[:, lo // PER_COLUMN : hi // PER_COLUMN]


def tile_list_raceway_noise_scores_kernel(
    tc, tab_words, tab_scales, offs, pos1, pos2, pos3, w1, w2_words, w2_scales, bias, unit, w3, gain, out
):
    nc = tc.nc
    with ExitStack() as ctx:
        keep = ctx.enter_context(tc.tile_pool(name="keep", bufs=1))
        ring = ctx.enter_context(tc.tile_pool(name="ring", bufs=2))
        psum = ctx.enter_context(tc.psum_pool(name="psum", bufs=4))

        idx = keep.tile([P, S // PER_COLUMN], U16, name="idx")
        p1 = keep.tile([P, PAIRS // PER_COLUMN], U16, name="p1")
        p2 = keep.tile([P, PAIRS // PER_COLUMN], U16, name="p2")
        p3 = keep.tile([P, S // PER_COLUMN], U16, name="p3")
        tab_w = keep.tile([P, T], U32, name="tab_w", align_bytes=64)
        tab_s = keep.tile([P, T], U8, name="tab_s", align_bytes=64)
        w2_w = keep.tile([P, 2 * H], U8, name="w2_w", align_bytes=64)
        w2_s = keep.tile([P, H], U8, name="w2_s", align_bytes=64)
        w1_raw = [
            [keep.tile([P, PACK, GROUP // 2], F32, name="w1_raw0%d" % u) for u in range(2)],
            [keep.tile([P, PACK, GROUP], F32, name="w1_raw1")],
        ]
        w3_raw = [
            [keep.tile([P, PACK, GROUP], F32, name="w3_raw%d%d" % (a, b)) for b in range(GROUPS)]
            for a in range(GROUPS)
        ]
        bias_c = keep.tile([P, GROUPS, PACK], F32, name="bias_c")
        unit_c = keep.tile([P, GROUPS, PACK], F32, name="unit_c")
        gain_c = keep.tile([P, GROUPS, PACK], F32, name="gain_c")

        tab_s_words = tab_s[:].bitcast(I32)
        nc.vector.memset(tab_s_words[:, 0 : T // 8], 0)
        nc.gpsimd.memset(tab_s_words[:, T // 8 : T // 4], 0)
        nc.vector.memset(w2_s[:].bitcast(I32), 0)

        w1_rows = w1.rearrange("(p j) c -> p j c", j=PACK)
        w3_rows = w3.rearrange("(a p j) c -> a p j c", p=P, j=PACK)

        load_scale_rows(nc, tab_s, tab_scales)
        nc.sync.dma_start(idx[:], offs)
        nc.sync.dma_start(p2[:], pos2)
        nc.sync.dma_start(p1[:], pos1)
        nc.sync.dma_start(out=w1_raw[0][0][:], in_=w1_rows[:, :, 0 : GROUP // 2])
        nc.sync.dma_start(out=w2_w[:].bitcast(I32), in_=w2_words[0].bitcast(I32))
        nc.sync.dma_start(out=bias_c[:], in_=bias.rearrange("(b p t) -> p b t", p=P, t=PACK))
        nc.sync.dma_start(
            out=tab_w[:].bitcast(I32), in_=tab_words[0].rearrange("p t i -> p (t i)").bitcast(I32)
        )
        nc.sync.dma_start(out=w1_raw[0][1][:], in_=w1_rows[:, :, GROUP // 2 : GROUP])
        load_scale_rows(nc, w2_s, w2_scales)
        nc.sync.dma_start(out=unit_c[:], in_=unit.rearrange("(b p t) -> p b t", p=P, t=PACK))
        nc.sync.dma_start(out=w1_raw[1][0][:], in_=w1_rows[:, :, GROUP:H])
        for b in range(GROUPS):
            for a in range(GROUPS):
                nc.sync.dma_start(out=w3_raw[a][b][:], in_=w3_rows[a, :, :, b * GROUP : (b + 1) * GROUP])
        nc.sync.dma_start(out=gain_c[:], in_=gain.rearrange("(b p t) -> p b t", p=P, t=PACK))
        nc.sync.dma_start(p3[:], pos3)

        w2_codes = keep.tile([P, 2 * H], U8, name="w2_codes", align_bytes=64)
        w2_plane = keep.tile([P, H], U8, name="w2_plane", align_bytes=64)
        v_s = keep.tile([P, S], U8, name="v_s", align_bytes=64)
        nc.vector.tensor_copy(v_s[:], tab_s[:].indirect(idx[:]))
        nc.vector.tensor_copy(
            out=w2_codes[:].rearrange("p (b t m e) -> p b t m e", b=GROUPS, t=PACK, e=2),
            in_=w2_w[:].rearrange("p (b m t e) -> p b t m e", b=GROUPS, t=PACK, e=2),
        )
        v_w = [keep.tile([P, BANK], U32, name="v_w%d" % half, align_bytes=64) for half in range(S // BANK)]
        nc.vector.tensor_copy(v_w[0][:], tab_w[:].indirect(entries(idx, 0, BANK)))
        nc.vector.tensor_copy(
            out=w2_plane[:].rearrange("p (b t m) -> p b t m", b=GROUPS, t=PACK),
            in_=w2_s[:].rearrange("p (b m t) -> p b t m", b=GROUPS, t=PACK),
        )
        nc.vector.tensor_copy(v_w[1][:], tab_w[:].indirect(entries(idx, BANK, S)))

        w1_q = {}

        def quantise_w1(b, pair):
            grouped = ring.tile([P, 2, GROUP], BF16, name="w1_grouped", align_bytes=64)
            codes = keep.tile([P, 2 * P], U32, name="w1_codes%d%d" % (b, pair), align_bytes=64)
            plane = keep.tile([P, 2 * P], U8, name="w1_plane%d%d" % (b, pair), align_bytes=64)
            width = GROUP // len(w1_raw[b])
            for u, raw in enumerate(w1_raw[b]):
                round_and_deal(nc, grouped[:, :, u * width : (u + 1) * width], raw, pair)
            nc.vector.quantize_mx(
                out=codes[:].bitcast(FP8X4), scales=plane[:], in_=grouped[:].rearrange("p t c -> p (t c)")
            )
            w1_q[b, pair] = (codes, plane)

        w3_grouped_tag = {(0, 0): "w3_first", (0, 1): "last_diff", (1, 0): "late0", (1, 1): "late1"}
        w3_q = {}
        w3_grouped = {}

        def round_w3(b, pair):
            grouped = keep.tile(
                [P, 2, GROUPS, GROUP], BF16, name="w3_grouped", tag=w3_grouped_tag[b, pair], align_bytes=64
            )
            for a in range(GROUPS):
                round_and_deal(nc, grouped[:, :, a, :], w3_raw[a][b], pair)
            w3_grouped[b, pair] = grouped

        def quantise_w3(i, count):
            b, t = divmod(i, PACK)
            width = GROUPS * P
            tag = ("late%d" if count == 1 else "w3_codes%d") % i
            codes = keep.tile([P, count * width], U32, name="w3_codes", tag=tag, align_bytes=64)
            plane = keep.tile([P, count * width], U8, name="w3_plane%d" % i, align_bytes=64)
            nc.vector.quantize_mx(
                out=codes[:].bitcast(FP8X4), scales=plane[:],
                in_=w3_grouped[b, t // 2][:, t % 2 : t % 2 + count, :, :].rearrange("p t a c -> p (t a c)"),
            )
            for u in range(count):
                w3_q[i + u] = (codes, plane, u * width)

        h = [keep.tile([P, S], F32, name="h%d" % i) for i in range(TILES)]
        z_rows = [keep.tile([P, PACK, PAIRS], BF16, name="z_rows%d" % b) for b in range(GROUPS)]

        sizes, signed = {}, {}

        def products(i):
            b, t = divmod(i, PACK)
            codes, plane = w1_q[b, t // 2]
            cols = slice((t % 2) * P, (t % 2 + 1) * P)
            sizes[i] = ring.tile([P, S], F32, name="size", bufs=4)
            for half in range(S // BANK):
                js = slice(half * BANK, (half + 1) * BANK)
                for_scalar = psum.tile([P, BANK], F32, name="for_scalar")
                signed[i, half] = psum.tile([P, BANK], F32, name="for_vector")
                nc.tensor.matmul_mx(
                    out=for_scalar[:], lhsT=codes[:, cols].bitcast(FP8X4), lhsT_scale=plane[:, cols],
                    rhs=v_w[half][:].bitcast(FP8X4), rhs_scale=v_s[:, js], start=True, stop=True,
                )
                nc.tensor.matmul_mx(
                    out=signed[i, half][:], lhsT=w2_codes[:, 2 * i * P : 2 * (i + 1) * P].bitcast(FP4X4),
                    lhsT_scale=w2_plane[:, i * P : (i + 1) * P],
                    rhs=v_w[half][:].bitcast(FP8X4), rhs_scale=v_s[:, js], start=True, stop=True,
                )
                nc.scalar.activation(out=sizes[i][:, js], in_=for_scalar[:], func=ACT.Abs)

        def add_up(i, half):
            b, t = divmod(i, PACK)
            js = slice(half * BANK, (half + 1) * BANK)
            nc.vector.scalar_tensor_tensor(
                out=h[i][:, js], in0=signed[i, half][:], scalar=bias_c[:, b, t : t + 1], in1=sizes[i][:, js],
                op0=ALU.add, op1=ALU.add,
            )

        def pick_outer(i, outer, ms):
            nc.vector.tensor_copy(outer, h[i][:].indirect(entries(p2, ms.start, ms.stop)))

        def distance(i, outer, diff, ms):
            b, t = divmod(i, PACK)
            square = ring.tile([P, ms.stop - ms.start], F32, name="square")
            nc.vector.tensor_tensor(diff, h[i][:].indirect(entries(p1, ms.start, ms.stop)), outer, ALU.subtract)
            nc.scalar.activation(out=square[:], in_=diff, func=ACT.Square)
            nc.scalar.activation(
                out=z_rows[b][:, t, ms], in_=square[:], func=ACT.Sqrt, bias=unit_c[:, b, t : t + 1]
            )

        z_grouped = [keep.tile([P, PAIRS, PACK], BF16, name="z_grouped%d" % a, align_bytes=64) for a in range(GROUPS)]
        z_codes = [keep.tile([P, PAIRS], U32, name="z_codes%d" % a, align_bytes=64) for a in range(GROUPS)]
        z_plane = [keep.tile([P, PAIRS], U8, name="z_plane%d" % a, align_bytes=64) for a in range(GROUPS)]

        def weave_z(copy, a, ms):
            copy(
                out=z_grouped[a][:, ms, :].rearrange("p (c i) t -> p c t i", i=4),
                in_=z_rows[a][:, :, ms].rearrange("p t (c i) -> p c t i", i=4),
            )

        def quantise_z(a, ms):
            nc.vector.quantize_mx(
                out=z_codes[a][:, ms].bitcast(FP8X4), scales=z_plane[a][:, ms],
                in_=z_grouped[a][:, ms, :].rearrange("p m t -> p (m t)"),
            )

        all_pairs = slice(0, PAIRS)
        half_pairs = (slice(0, PAIRS // 2), slice(PAIRS // 2, PAIRS))

        quantise_w1(0, 0)
        quantise_w1(0, 1)
        products(0)
        products(1)
        add_up(0, 0)
        add_up(0, 1)
        for i in range(TILES - 1):
            if i + 2 < TILES:
                products(i + 2)
            outer, diff = sizes[i + 1][:, 0:PAIRS], sizes[i + 1][:, PAIRS:S]
            add_up(i + 1, 0)
            pick_outer(i, outer, all_pairs)
            add_up(i + 1, 1)
            distance(i, outer, diff, all_pairs)
            if i in (0, 2):
                quantise_w1(1, i // 2)
            if i == PACK - 1:
                round_w3(0, 0)
            if i + 2 == TILES - 1:
                weave_z(nc.scalar.copy, 0, all_pairs)
                quantise_z(0, all_pairs)
        for u, ms in enumerate(half_pairs):
            outer = keep.tile([P, PAIRS // 2], F32, name="outer", tag="late%d" % u, align_bytes=64)
            diff = keep.tile([P, PAIRS // 2], F32, name="diff", tag=("diff", "last_diff")[u], align_bytes=64)
            pick_outer(TILES - 1, outer[:], ms)
            distance(TILES - 1, outer[:], diff[:], ms)
        weave_z(nc.vector.tensor_copy, 1, half_pairs[0])
        quantise_w3(0, 1)
        weave_z(nc.vector.tensor_copy, 1, half_pairs[1])
        quantise_z(1, half_pairs[0])
        quantise_z(1, half_pairs[1])

        out_rows = out.rearrange("(b p t) j -> b t p j", p=P, t=PACK)
        quarters = tuple((u * S // 4, (u + 1) * S // 4) for u in range(4))
        halves = ((0, S // 2), (S // 2, S))
        taper = halves[:1] + quarters[2:]
        scores = keep.tile([P, TILES * PAIRS], F32, name="scores")
        picked = {}

        def second_product(i, parts):
            codes, plane, start = w3_q[i]
            at = (TILES - 1 - i) * PAIRS
            for ms in parts:
                acc = psum.tile([P, ms.stop - ms.start], F32, name="for_scalar")
                for a in range(GROUPS):
                    cols = slice(start + a * P, start + (a + 1) * P)
                    nc.tensor.matmul_mx(
                        out=acc[:], lhsT=codes[:, cols].bitcast(FP8X4), lhsT_scale=plane[:, cols],
                        rhs=z_codes[a][:, ms].bitcast(FP8X4), rhs_scale=z_plane[a][:, ms],
                        start=(a == 0), stop=(a == GROUPS - 1),
                    )
                nc.scalar.copy(out=scores[:, at + ms.start : at + ms.stop], in_=acc[:])

        def pick(i, lo, hi):
            at = (TILES - 1 - i) * PAIRS
            window = scores[:, at : min(at + 2 * PAIRS, TILES * PAIRS)]
            nc.vector.tensor_copy(picked[i][:, lo:hi], window.indirect(entries(p3, lo, hi)))

        def cap_and_store(i, lo, hi):
            b, t = divmod(i, PACK)
            result = ring.tile([P, hi - lo], F32, name="result", bufs=4)
            nc.vector.scalar_tensor_tensor(
                out=result[:], in0=h[i][:, lo:hi], scalar=gain_c[:, b, t : t + 1], in1=picked[i][:, lo:hi],
                op0=ALU.mult, op1=ALU.min,
            )
            nc.sync.dma_start(out=out_rows[b, t, :, lo:hi], in_=result[:])

        second_product(0, half_pairs)
        quantise_w3(1, 1)
        second_product(1, (all_pairs,))
        round_w3(0, 1)
        for i in range(TILES):
            slices = quarters if i == 0 else taper if i == TILES - 1 else halves
            picked[i] = ring.tile([P, S], F32, name="picked")
            pick(i, *slices[0])
            if i >= 1:
                cap_and_store(i - 1, 0, S)
            if i + 2 < TILES:
                if i % 2 == 0:
                    quantise_w3(i + 2, 2)
                second_product(i + 2, (all_pairs,))
            if i < 2:
                round_w3(1, i)
            pick(i, *slices[1])
            if i == TILES - 1:
                cap_and_store(i, *slices[0])
            for part in slices[2:]:
                pick(i, *part)
        for part in taper[1:]:
            cap_and_store(TILES - 1, *part)
